import numpy as np, ml_dtypes
CORES = [120,124,248,252,376,380,504,508]
N = 8
T, SQ = 4096, 2048
def entries(a): return a.T.reshape(-1)
def pack(v, P): return np.ascontiguousarray(np.asarray(v, np.int32).reshape(-1, P).T)
def lists(rng, how):
    d = np.concatenate([[0], rng.integers(1 - SQ // 2, SQ // 2, N - 1), [int(rng.integers(1 - SQ // 2, 1))]])
    if how == "lag": d[1:] = -SQ
    if how == "lead": d[1:N] = SQ; d[N] = 0
    if how == "runs": m = int(rng.integers(1, N - 2)); d[m] = -abs(d[m]); d[m + 1] = d[m] + SQ; d[m + 2] = d[m]
    if how == "skew": t = int(rng.integers(2, N - 1)); d[1:] = rng.integers(SQ // 2 + 1, SQ - 1, N); d[t + 1:] *= -1; d[t] = d[t - 1] + d[t + 1]
    n = SQ + np.diff(d)
    F = np.zeros((N, T), np.int64)
    for r in range(N):
        o = rng.permutation(T)
        if how == "runs": o = (T // 16 * rng.permutation(16)[:, None] + np.arange(T // 16)).reshape(-1)
        if how == "skew": o = np.concatenate([[0, T - 1], 1 + rng.permutation(T - 2)])
        F[r, o[:n[r]]] = 1
    return {"fl": np.stack([pack(f, 16) for f in F])}
def setup_inputs(rng):
    return dict({"x": rng.standard_normal((N, 128, T), dtype=np.float32).astype(ml_dtypes.bfloat16), "st": rng.standard_normal((N, 128, SQ), dtype=np.float32).astype(ml_dtypes.bfloat16)}, **lists(rng, "uniform"))
def setup_inputs_lag(rng):
    d = setup_inputs(rng); d.update(lists(rng, "lag"))
    for k in ("x", "st"): d[k] = (d[k].astype(np.float32) * 1048576.0).astype(d[k].dtype)
    return d
def setup_inputs_lead(rng):
    d = setup_inputs(rng); d.update(lists(rng, "lead"))
    for k in ("x", "st"): d[k] = (d[k].astype(np.float32) * (1 / 1024.0)).astype(d[k].dtype)
    return d
def setup_inputs_runs(rng):
    d = setup_inputs(rng); d.update(lists(rng, "runs"))
    return d
def setup_inputs_skew(rng):
    d = setup_inputs(rng); d.update(lists(rng, "skew"))
    return d
def check_inputs(x):
    bad = []
    if x["fl"].min() < 0 or x["fl"].max() >= 2: bad.append("fl out of range")
    if int(x["fl"].sum()) > N * SQ: bad.append("more flags than the stream has columns")
    c = np.concatenate([[0], np.cumsum([int(a.sum()) for a in x["fl"]])])
    if any(c[r] < (r - 1) * SQ or c[r + 1] > (r + 2) * SQ for r in range(N)): bad.append("a rank's share of the stream reaches beyond its neighbours' parts")
    return bad
def reference(x, st, fl):
    S = np.concatenate(list(st), axis=1); X = np.concatenate(list(x), axis=1)
    F = np.concatenate([entries(f) for f in fl]) > 0; c = np.cumsum(F) - F
    Y = np.where(F[None, :], S[:, np.minimum(c, N * SQ - 1)], X)
    return {"y": np.stack([Y[:, T * r:T * r + T] for r in range(N)])}

@@ -1,0 +1,299 @@
+import numpy as np
+from concourse.bass import DstId, RemoteDMATransfer
+from concourse.mybir import dt, AluOpType, AxisListType, ActivationFunctionType
+
+T_, SQ, NR = 4096, 2048, 8
+PIECE = 256
+CUTS = [48, 48, 32]
+
+SCRATCH = {
+    "win": ("sbuf", [128, T_ + 3 * SQ], "bfloat16"),
+    "yb": ("sbuf", [128, T_], "bfloat16"),
+    "fi": ("sbuf", [16, 256], "int32"),
+    "fb": ("sbuf", [16, 256], "bfloat16"),
+    "one": ("sbuf", [16, 128], "bfloat16"),
+    "neg": ("sbuf", [16, 128], "bfloat16"),
+    "rep": ("sbuf", [16, 128], "bfloat16"),
+    "low": ("sbuf", [16, 128], "bfloat16"),
+    "zero": ("sbuf", [128, 256], "float32"),
+    "jq": ("sbuf", [128, 256], "float32"),
+    "jj": ("sbuf", [128, 256], "float32"),
+    "jk": ("sbuf", [128, 256], "float32"),
+    "pi": ("sbuf", [128, 8], "int32"),
+    "pj": ("sbuf", [128, 8], "int32"),
+    "pf": ("sbuf", [128, 8], "float32"),
+    "cs": ("sbuf", [128, 256], "float32"),
+    "uu": ("sbuf", [128, 256], "float32"),
+    "uv": ("sbuf", [128, 256], "float32"),
+    "vv": ("sbuf", [128, 256], "float32"),
+    "ww": ("sbuf", [128, 256], "float32"),
+    "tt": ("sbuf", [128, 256], "float32"),
+    "of": ("sbuf", [128, 256], "float32"),
+    "off": ("sbuf", [128, 256], "uint16"),
+    "cnt": ("sbuf", [128, 8], "float32"),
+    "bc": ("sbuf", [128, 8], "float32"),
+    "psc": ("psum", [128, 512], "float32"),
+    "psf": ("psum", [128, 512], "float32"),
+    "pst": ("psum", [128, 512], "float32"),
+}
+SEMAPHORES = ["lf", "lh", "ld", "lx1", "lx2", "gate", "sent", "data", "hin", "cin",
+              "vone", "v", "gs", "gj", "fbs", "pcs", "pts", "css", "offs",
+              "gv0", "gv1", "gv2", "ga0", "ga1", "ga2", "sy", "sz"]
+
+
+def bits(m):
+    return [i for i in range(16) if m >> i & 1]
+
+
+def tomask(b):
+    return int(sum(1 << i for i in b))
+
+
+def here(topo, a, b):
+    return topo.host(a) == topo.host(b) and topo.chip(a) == topo.chip(b)
+
+
+def helpers(T, topo, r):
+    chip = [c for c in range(512) if here(topo, c, T.cores[r])]
+    ranks = [c for c in chip if T.rank_of(c) is not None]
+    free = [c for c in chip if T.rank_of(c) is None]
+    return free[1 - ranks.index(T.cores[r])::2]
+
+
+def far(T, topo, r):
+    for q in (r - 1, r + 1):
+        if 0 <= q < NR and not here(topo, T.cores[q], T.cores[r]):
+            return q
+    return None
+
+
+def near(T, topo, r):
+    for q in (r - 1, r + 1):
+        if 0 <= q < NR and here(topo, T.cores[q], T.cores[r]):
+            return q
+    return None
+
+
+def slot(r, i):
+    return T_ + (i - max(r - 1, 0)) * SQ
+
+
+def relay(T, topo, s):
+    hard = [T.cores[q] for q in range(s + 1, NR) if not topo.may_write(T.cores[s], T.cores[q])]
+    if not hard:
+        return None
+    for e in range(NR):
+        if far(T, topo, e) is None:
+            x = helpers(T, topo, e)[0]
+            if topo.may_write(T.cores[s], x) and all(topo.may_write(x, d) for d in hard):
+                return x, [q for q in range(s + 1, NR) if T.cores[q] in hard or here(topo, x, T.cores[q])]
+    return None
+
+
+def count_dsts(T, topo, s):
+    rel = relay(T, topo, s)
+    if rel is None:
+        return [T.cores[q] for q in range(s + 1, NR)]
+    return [T.cores[q] for q in range(s + 1, NR) if q not in rel[1]] + [rel[0]]
+
+
+def engines(topo, a, b):
+    chip = [c for c in range(512) if here(topo, c, a)]
+    on = topo.mask(a, [c for c in chip if c != a][0])
+    away = [c for c in range(512) if not here(topo, c, a) and topo.may_write(a, c)]
+    out = topo.mask(a, away[0])
+    return (on & ~out) if here(topo, a, b) else out
+
+
+def fan_out(g, T, topo, core, src, dsts, col, nsent):
+    tr = []
+    for on in (False, True):
+        ds = [d for d in dsts if here(topo, core, d) == on]
+        if ds:
+            m = engines(topo, core, ds[0])
+            ids = []
+            for d in ds:
+                rid, pid = topo.addr(d, core)
+                ids.append(DstId(rid=rid, pnc=pid))
+            tr.append(RemoteDMATransfer(dst_ids=ids, dma_engine_mask=m, remote_sem=T.sem.cin, srcs=[src],
+                                        dsts=[T.cnt[:, col[0]:col[1]] for d in ds]))
+            nsent[0] += len(bits(m))
+    g.remote_dma_fused(tr, local_sem=T.sem.sent)
+
+
+def rank_program(g, core, T, topo):
+    rank = T.rank_of(core)
+    if rank is None:
+        helper_program(g, core, T, topo)
+        return
+    S, A, V, PE = T.sem, AluOpType, g.vector, g.tensor
+    fr, nr = far(T, topo, rank), near(T, topo, rank)
+    own = slot(rank, rank)
+    first = max(rank - 1, 0)
+    nparts = min(rank + 1, NR - 1) - first + 1
+    end = T_ + nparts * SQ
+    hp = helpers(T, topo, rank)
+    nh = PIECE * len(hp) if fr is not None else 0
+    off_eng = None if fr is None else topo.mask(core, T.cores[fr])
+    nsent = [0]
+
+    g.sync.dma_start(T.fi[:], T.fl[:]).then_inc(S.lf, 16)
+    if nh:
+        g.scalar.dma_start(T.win[:, own:own + nh], T.st[:, 0:nh]).then_inc(S.lh, 16)
+        g.sync.dma_start(T.win[:, own + nh:own + SQ], T.st[:, nh:SQ]).then_inc(S.ld, 16)
+    else:
+        g.scalar.dma_start(T.win[:, own:own + SQ], T.st[:, 0:SQ]).then_inc(S.ld, 16)
+    g.scalar.dma_start(T.win[:, 0:SQ], T.x[:, 0:SQ]).then_inc(S.lx1, 16)
+    g.sync.wait_ge(S.gate, 1)
+    g.sync.dma_start(T.win[:, SQ:T_], T.x[:, SQ:T_]).then_inc(S.lx2, 16)
+
+    V.memset(T.one[:], 1.0).then_inc(S.vone, 1)
+    V.memset(T.neg[:], -1.0).then_inc(S.vone, 1)
+    V.memset(T.zero[:], 0.0).then_inc(S.v, 1)
+    g.wait_ge(S.vone, 2)
+    g.affine_select(T.rep[:], T.one[:], [[0, 8], [-1, 16]], A.is_equal, 0.0, 0, 1).then_inc(S.gs, 1)
+    g.affine_select(T.low[:], T.neg[:], [[0, 8], [-1, 16]], A.is_ge, 0.0, 0, 1).then_inc(S.gs, 1)
+    g.iota(T.pi[:, 0:1], [[0, 1]], 0, 1).then_inc(S.gj, 1)
+    g.iota(T.jq[:], [[16, 256]], 0, 0, allow_small_or_imprecise_dtypes=True).then_inc(S.gj, 1)
+
+    V.wait_ge(S.lf, 16)
+    V.tensor_copy(T.fb[:], T.fi[:]).then_inc(S.fbs, 1)
+    PE.wait_ge(S.vone, 2)
+    PE.wait_ge(S.fbs, 1)
+    PE.matmul(T.psc[:, 0:256], T.one[:], T.fb[:], True, True).then_inc(S.pcs, 1)
+    PE.wait_ge(S.gs, 2)
+    PE.matmul(T.psf[:, 0:256], T.rep[:], T.fb[:], True, True).then_inc(S.pts, 1)
+    PE.matmul(T.pst[:, 0:256], T.low[:], T.fb[:], True, True).then_inc(S.pts, 1)
+    V.wait_ge(S.v, 1)
+    V.wait_ge(S.pcs, 1)
+    V.tensor_tensor_scan(T.cs[:], T.psc[:, 0:256], T.zero[:], 0.0, A.add, A.add).then_inc(S.css, 1)
+
+    if nh:
+        g.wait_ge(S.lh, 16)
+        on = bits(topo.mask(core, hp[0]))
+        tr = []
+        for k, h in enumerate(hp):
+            rid, pid = topo.addr(h, core)
+            e = on[(k + 1) * 4:(k + 2) * 4]
+            tr.append(RemoteDMATransfer(dst_ids=[DstId(rid=rid, pnc=pid)], dma_engine_mask=tomask(e), remote_sem=S.hin,
+                                        srcs=[T.win[:, own + k * PIECE:own + (k + 1) * PIECE]], dsts=[T.win[:, 0:PIECE]]))
+            nsent[0] += len(e)
+        g.remote_dma_fused(tr, local_sem=S.sent)
+    g.wait_ge(S.css, 1)
+    dsts = count_dsts(T, topo, rank)
+    if dsts:
+        fan_out(g, T, topo, core, T.cs[:, 255:256], dsts, (rank, rank + 1), nsent)
+    g.wait_ge(S.ld, 16)
+    if fr is not None:
+        rid, pid = topo.addr(T.cores[fr], core)
+        to = slot(fr, rank)
+        g.remote_dma(T.win[:, to + nh:to + SQ], T.win[:, own + nh:own + SQ], S.data, S.sent, pid, rid, off_eng)
+        nsent[0] += len(bits(off_eng))
+    g.sem_inc(S.gate, 1)
+    rid, pid = topo.addr(T.cores[nr], core)
+    to = slot(nr, rank)
+    m = near_mask(T, topo, rank)
+    g.remote_dma(T.win[:, to:to + SQ], T.win[:, own:own + SQ], S.data, S.sent, pid, rid, m)
+    nsent[0] += len(bits(m))
+
+    K = T_ - SQ * first
+    V.wait_ge(S.gj, 2)
+    V.tensor_scalar(T.pj[:, 0:1], T.pi[:, 0:1], 15, None, A.bitwise_and).then_inc(S.v, 1)
+    V.wait_ge(S.v, 2)
+    V.tensor_copy(T.pf[:, 0:1], T.pj[:, 0:1]).then_inc(S.v, 1)
+    V.wait_ge(S.v, 3)
+    V.tensor_scalar(T.jj[:], T.jq[:], T.pf[:, 0:1], None, A.add).then_inc(S.v, 1)
+    V.tensor_scalar(T.jk[:], T.jq[:], T.pf[:, 0:1], float(-K), A.add, A.add).then_inc(S.v, 1)
+    V.wait_ge(S.v, 5)
+    V.wait_ge(S.pts, 2)
+    V.wait_ge(S.css, 1)
+    V.tensor_tensor(T.uu[:], T.pst[:, 0:256], T.jk[:], A.subtract).then_inc(S.v, 1)
+    V.wait_ge(S.v, 6)
+    V.tensor_tensor(T.uv[:], T.uu[:], T.cs[:], A.add).then_inc(S.v, 1)
+    V.wait_ge(S.v, 7)
+    V.tensor_tensor(T.vv[:], T.uv[:], T.psf[:, 0:256], A.mult).then_inc(S.v, 1)
+    V.wait_ge(S.v, 8)
+    V.tensor_tensor(T.ww[:], T.vv[:], T.jj[:], A.add).then_inc(S.v, 1)
+    V.wait_ge(S.v, 9)
+    if rank == 0:
+        V.tensor_copy(T.off[:], T.ww[:]).then_inc(S.offs, 1)
+    else:
+        need = 0
+        for s in range(rank):
+            rel = relay(T, topo, s)
+            if rel is None or rank not in rel[1]:
+                need += len(bits(engines(topo, T.cores[s], core)))
+        for x in sorted({relay(T, topo, s)[0] for s in range(rank) if relay(T, topo, s) and rank in relay(T, topo, s)[1]}):
+            need += len(bits(engines(topo, x, core)))
+        V.wait_ge(S.cin, need)
+        V.tensor_reduce(T.bc[:, 0:1], T.cnt[:, 0:rank], AxisListType.X, A.add).then_inc(S.v, 1)
+        V.wait_ge(S.v, 10)
+        V.tensor_scalar(T.tt[:], T.psf[:, 0:256], T.bc[:, 0:1], None, A.mult).then_inc(S.v, 1)
+        V.wait_ge(S.v, 11)
+        V.tensor_tensor(T.of[:], T.tt[:], T.ww[:], A.add).then_inc(S.v, 1)
+        V.wait_ge(S.v, 12)
+        V.tensor_copy(T.off[:], T.of[:]).then_inc(S.offs, 1)
+
+    ndata = len(bits(near_mask(T, topo, nr)))
+    if fr is not None:
+        ndata += len(bits(topo.mask(T.cores[fr], core)))
+        ndata += sum(len(pass_on(topo, h, core)) for h in helpers(T, topo, fr))
+    for q in (V, g.scalar):
+        q.wait_ge(S.ld, 16)
+        if nh:
+            q.wait_ge(S.lh, 16)
+        q.wait_ge(S.lx1, 16)
+        q.wait_ge(S.lx2, 16)
+        q.wait_ge(S.offs, 1)
+        q.wait_ge(S.data, ndata)
+    k0 = 0
+    cuts = []
+    for i, w in enumerate(CUTS):
+        for q in ("gv", "ga"):
+            cuts.append((q, i, k0, k0 + w))
+            k0 += w
+    last = cuts[-1]
+    for c in cuts:
+        q, i, a, b = c
+        src = T.win[:, 0:end].indirect(T.off[:, a:b])
+        if q == "gv":
+            V.tensor_copy(T.yb[:, 16 * a:16 * b], src).then_inc(S["gv%d" % i], 1)
+        else:
+            g.scalar.activation(T.yb[:, 16 * a:16 * b], src, ActivationFunctionType.Copy).then_inc(S["ga%d" % i], 1)
+        qq, sm = (g.scalar, S.sz) if c == last else (g.sync, S.sy)
+        qq.wait_ge(S["%s%d" % (q, i)], 1)
+        qq.dma_start(T.y[:, 16 * a:16 * b], T.yb[:, 16 * a:16 * b]).then_inc(sm, 16)
+    g.scalar.wait_ge(S.sz, 16)
+    g.sync.wait_ge(S.sy, 16 * (len(cuts) - 1))
+    g.wait_ge(S.sent, nsent[0])
+
+
+def near_mask(T, topo, r):
+    a, b = T.cores[r], T.cores[near(T, topo, r)]
+    return topo.mask(a, b) if far(T, topo, r) is None else engines(topo, a, b)
+
+
+def pass_on(topo, h, dst):
+    return bits(topo.mask(h, dst))[::2]
+
+
+def helper_program(g, core, T, topo):
+    S = T.sem
+    nsent = [0]
+    for r in range(NR):
+        fr = far(T, topo, r)
+        if fr is not None and here(topo, core, T.cores[r]) and core in helpers(T, topo, r):
+            k = helpers(T, topo, r).index(core)
+            to = slot(fr, r) + k * PIECE
+            e = pass_on(topo, core, T.cores[fr])
+            rid, pid = topo.addr(T.cores[fr], core)
+            g.wait_ge(S.hin, 4)
+            g.remote_dma(T.win[:, to:to + PIECE], T.win[:, 0:PIECE], S.data, S.sent, pid, rid, tomask(e))
+            nsent[0] += len(e)
+    src = [s for s in range(NR) if relay(T, topo, s) is not None and relay(T, topo, s)[0] == core]
+    if src:
+        g.wait_ge(S.cin, sum(len(bits(engines(topo, T.cores[s], core))) for s in src))
+        a, b = src[0], src[-1] + 1
+        fan_out(g, T, topo, core, T.cnt[:, a:b], [T.cores[q] for q in relay(T, topo, src[0])[1]], (a, b), nsent)
+    if nsent[0]:
+        g.wait_ge(S.sent, nsent[0])

@@ -3,8 +3,8 @@ from concourse.bass import DstId, RemoteDMATransfer
 from concourse.mybir import dt, AluOpType, AxisListType, ActivationFunctionType
 
 T_, SQ, NR = 4096, 2048, 8
-PIECE = 256
-CUTS = [48, 48, 32]
+PC, PS = 384, 256
+CUTS = [40, 48, 40]
 
 SCRATCH = {
     "win": ("sbuf", [128, T_ + 3 * SQ], "bfloat16"),
@@ -36,7 +36,7 @@ SCRATCH = {
     "psf": ("psum", [128, 512], "float32"),
     "pst": ("psum", [128, 512], "float32"),
 }
-SEMAPHORES = ["lf", "lh", "ld", "lx1", "lx2", "gate", "sent", "data", "hin", "cin",
+SEMAPHORES = ["lf", "lh", "ld", "lx1", "lx2", "gate", "sent", "data", "hin", "c0", "c1", "c2", "c3",
               "vone", "v", "gs", "gj", "fbs", "pcs", "pts", "css", "offs",
               "gv0", "gv1", "gv2", "ga0", "ga1", "ga2", "sy", "sz"]
 
@@ -53,25 +53,27 @@ def here(topo, a, b):
     return topo.host(a) == topo.host(b) and topo.chip(a) == topo.chip(b)
 
 
-def helpers(T, topo, r):
-    chip = [c for c in range(512) if here(topo, c, T.cores[r])]
+def neighbours(T, topo, r):
+    f = n = None
+    for q in (r - 1, r + 1):
+        if 0 <= q < NR:
+            if here(topo, T.cores[q], T.cores[r]):
+                n = q
+            else:
+                f = q
+    return f, n
+
+
+def split(T, topo, r):
+    f = neighbours(T, topo, r)[0]
+    if f is None:
+        return []
+    me, to = T.cores[r], T.cores[f]
+    w = PS if topo.rack(topo.host(me)) == topo.rack(topo.host(to)) else PC
+    chip = [c for c in range(512) if here(topo, c, me)]
     ranks = [c for c in chip if T.rank_of(c) is not None]
-    free = [c for c in chip if T.rank_of(c) is None]
-    return free[1 - ranks.index(T.cores[r])::2]
-
-
-def far(T, topo, r):
-    for q in (r - 1, r + 1):
-        if 0 <= q < NR and not here(topo, T.cores[q], T.cores[r]):
-            return q
-    return None
-
-
-def near(T, topo, r):
-    for q in (r - 1, r + 1):
-        if 0 <= q < NR and here(topo, T.cores[q], T.cores[r]):
-            return q
-    return None
+    free = [c for c in chip if T.rank_of(c) is None][1 - ranks.index(me)::2]
+    return [(h, k * w, k * w + w, bits(topo.mask(h, to))[::2]) for k, h in enumerate(free)]
 
 
 def slot(r, i):
@@ -79,46 +81,51 @@ def slot(r, i):
 
 
 def relay(T, topo, s):
-    hard = [T.cores[q] for q in range(s + 1, NR) if not topo.may_write(T.cores[s], T.cores[q])]
-    if not hard:
-        return None
+    hard = [q for q in range(s + 1, NR) if not topo.may_write(T.cores[s], T.cores[q])]
+    if hard:
+        for e in range(NR):
+            x = T.cores[e]
+            if (neighbours(T, topo, e)[0] is None and topo.may_write(T.cores[s], x)
+                    and all(topo.may_write(x, T.cores[d]) for d in hard)):
+                return e, [q for q in range(s + 1, NR) if q in hard or q != e and here(topo, x, T.cores[q])]
+    return None, []
+
+
+def messages(T, topo):
+    ms = []
+    for s in range(NR - 1):
+        e, served = relay(T, topo, s)
+        straight = [q for q in range(s + 1, NR) if q not in served and q != e]
+        ms.append((s, ([] if e is None else [e]) + straight, s, s + 1))
     for e in range(NR):
-        if far(T, topo, e) is None:
-            x = helpers(T, topo, e)[0]
-            if topo.may_write(T.cores[s], x) and all(topo.may_write(x, d) for d in hard):
-                return x, [q for q in range(s + 1, NR) if T.cores[q] in hard or here(topo, x, T.cores[q])]
-    return None
+        src = [s for s in range(NR) if relay(T, topo, s)[0] == e]
+        if src:
+            ms.append((e, sorted(relay(T, topo, src[-1])[1]), src[0], src[-1] + 1))
+    return ms
 
 
-def count_dsts(T, topo, s):
-    rel = relay(T, topo, s)
-    if rel is None:
-        return [T.cores[q] for q in range(s + 1, NR)]
-    return [T.cores[q] for q in range(s + 1, NR) if q not in rel[1]] + [rel[0]]
+def leaving(topo, a):
+    return topo.mask(a, [c for c in range(512) if not here(topo, c, a) and topo.may_write(a, c)][0])
 
 
-def engines(topo, a, b):
-    chip = [c for c in range(512) if here(topo, c, a)]
-    on = topo.mask(a, [c for c in chip if c != a][0])
-    away = [c for c in range(512) if not here(topo, c, a) and topo.may_write(a, c)]
-    out = topo.mask(a, away[0])
-    return (on & ~out) if here(topo, a, b) else out
+def staying(T, topo, r):
+    a, b = T.cores[r], T.cores[neighbours(T, topo, r)[1]]
+    return topo.mask(a, b) & ~leaving(topo, a)
 
 
-def fan_out(g, T, topo, core, src, dsts, col, nsent):
-    tr = []
-    for on in (False, True):
-        ds = [d for d in dsts if here(topo, core, d) == on]
-        if ds:
-            m = engines(topo, core, ds[0])
-            ids = []
-            for d in ds:
-                rid, pid = topo.addr(d, core)
-                ids.append(DstId(rid=rid, pnc=pid))
-            tr.append(RemoteDMATransfer(dst_ids=ids, dma_engine_mask=m, remote_sem=T.sem.cin, srcs=[src],
-                                        dsts=[T.cnt[:, col[0]:col[1]] for d in ds]))
-            nsent[0] += len(bits(m))
-    g.remote_dma_fused(tr, local_sem=T.sem.sent)
+def csem(T, topo, s):
+    return T.sem["c%d" % topo.host(T.cores[s])]
+
+
+def tell(g, T, topo, core, src, msg):
+    m = leaving(topo, core)
+    ids = []
+    for q in msg[1]:
+        rid, pid = topo.addr(T.cores[q], core)
+        ids.append(DstId(rid=rid, pnc=pid))
+    g.remote_dma_fused([RemoteDMATransfer(dst_ids=ids, dma_engine_mask=m, remote_sem=csem(T, topo, msg[2]), srcs=[src],
+                                          dsts=[T.cnt[:, msg[2]:msg[3]] for q in ids])], local_sem=T.sem.sent)
+    return len(bits(m))
 
 
 def rank_program(g, core, T, topo):
@@ -127,22 +134,25 @@ def rank_program(g, core, T, topo):
         helper_program(g, core, T, topo)
         return
     S, A, V, PE = T.sem, AluOpType, g.vector, g.tensor
-    fr, nr = far(T, topo, rank), near(T, topo, rank)
+    fr, nr = neighbours(T, topo, rank)
     own = slot(rank, rank)
     first = max(rank - 1, 0)
     nparts = min(rank + 1, NR - 1) - first + 1
     end = T_ + nparts * SQ
-    hp = helpers(T, topo, rank)
-    nh = PIECE * len(hp) if fr is not None else 0
-    off_eng = None if fr is None else topo.mask(core, T.cores[fr])
-    nsent = [0]
+    pieces = split(T, topo, rank)
+    nh = pieces[-1][2] if pieces else 0
+    nsent = 0
+    ms = messages(T, topo)
+    cwait = {}
+    for m in ms:
+        if rank in m[1]:
+            h = topo.host(T.cores[m[2]])
+            cwait[h] = cwait.get(h, 0) + len(bits(leaving(topo, T.cores[m[0]])))
 
     g.sync.dma_start(T.fi[:], T.fl[:]).then_inc(S.lf, 16)
-    if nh:
-        g.scalar.dma_start(T.win[:, own:own + nh], T.st[:, 0:nh]).then_inc(S.lh, 16)
-        g.sync.dma_start(T.win[:, own + nh:own + SQ], T.st[:, nh:SQ]).then_inc(S.ld, 16)
-    else:
-        g.scalar.dma_start(T.win[:, own:own + SQ], T.st[:, 0:SQ]).then_inc(S.ld, 16)
+    cut = nh if nh else SQ // 2
+    g.scalar.dma_start(T.win[:, own:own + cut], T.st[:, 0:cut]).then_inc(S.lh, 16)
+    g.sync.dma_start(T.win[:, own + cut:own + SQ], T.st[:, cut:SQ]).then_inc(S.ld, 16)
     g.scalar.dma_start(T.win[:, 0:SQ], T.x[:, 0:SQ]).then_inc(S.lx1, 16)
     g.sync.wait_ge(S.gate, 1)
     g.sync.dma_start(T.win[:, SQ:T_], T.x[:, SQ:T_]).then_inc(S.lx2, 16)
@@ -168,33 +178,35 @@ def rank_program(g, core, T, topo):
     V.wait_ge(S.pcs, 1)
     V.tensor_tensor_scan(T.cs[:], T.psc[:, 0:256], T.zero[:], 0.0, A.add, A.add).then_inc(S.css, 1)
 
-    if nh:
-        g.wait_ge(S.lh, 16)
-        on = bits(topo.mask(core, hp[0]))
+    g.wait_ge(S.lh, 16)
+    if pieces:
+        on = bits(topo.mask(core, pieces[0][0]))
         tr = []
-        for k, h in enumerate(hp):
+        for k, (h, a, b, e) in enumerate(pieces):
             rid, pid = topo.addr(h, core)
-            e = on[(k + 1) * 4:(k + 2) * 4]
-            tr.append(RemoteDMATransfer(dst_ids=[DstId(rid=rid, pnc=pid)], dma_engine_mask=tomask(e), remote_sem=S.hin,
-                                        srcs=[T.win[:, own + k * PIECE:own + (k + 1) * PIECE]], dsts=[T.win[:, 0:PIECE]]))
-            nsent[0] += len(e)
+            q = on[(k + 1) * 4:(k + 2) * 4]
+            tr.append(RemoteDMATransfer(dst_ids=[DstId(rid=rid, pnc=pid)], dma_engine_mask=tomask(q), remote_sem=S.hin,
+                                        srcs=[T.win[:, own + a:own + b]], dsts=[T.win[:, a:b]]))
+            nsent += len(q)
         g.remote_dma_fused(tr, local_sem=S.sent)
-    g.wait_ge(S.css, 1)
-    dsts = count_dsts(T, topo, rank)
-    if dsts:
-        fan_out(g, T, topo, core, T.cs[:, 255:256], dsts, (rank, rank + 1), nsent)
+    for m in ms:
+        if m[0] == rank and m[2] == rank:
+            g.wait_ge(S.css, 1)
+            nsent += tell(g, T, topo, core, T.cs[:, 255:256], m)
     g.wait_ge(S.ld, 16)
-    if fr is not None:
-        rid, pid = topo.addr(T.cores[fr], core)
-        to = slot(fr, rank)
-        g.remote_dma(T.win[:, to + nh:to + SQ], T.win[:, own + nh:own + SQ], S.data, S.sent, pid, rid, off_eng)
-        nsent[0] += len(bits(off_eng))
+    for q in (fr, nr):
+        if q is not None:
+            m = topo.mask(core, T.cores[q]) if q == fr else staying(T, topo, rank)
+            a = nh if q == fr else 0
+            rid, pid = topo.addr(T.cores[q], core)
+            to = slot(q, rank)
+            g.remote_dma(T.win[:, to + a:to + SQ], T.win[:, own + a:own + SQ], S.data, S.sent, pid, rid, m)
+            nsent += len(bits(m))
     g.sem_inc(S.gate, 1)
-    rid, pid = topo.addr(T.cores[nr], core)
-    to = slot(nr, rank)
-    m = near_mask(T, topo, rank)
-    g.remote_dma(T.win[:, to:to + SQ], T.win[:, own:own + SQ], S.data, S.sent, pid, rid, m)
-    nsent[0] += len(bits(m))
+    for m in ms:
+        if m[0] == rank and m[2] != rank:
+            g.wait_ge(csem(T, topo, m[2]), cwait[topo.host(T.cores[m[2]])])
+            nsent += tell(g, T, topo, core, T.cnt[:, m[2]:m[3]], m)
 
     K = T_ - SQ * first
     V.wait_ge(S.gj, 2)
@@ -218,14 +230,8 @@ def rank_program(g, core, T, topo):
     if rank == 0:
         V.tensor_copy(T.off[:], T.ww[:]).then_inc(S.offs, 1)
     else:
-        need = 0
-        for s in range(rank):
-            rel = relay(T, topo, s)
-            if rel is None or rank not in rel[1]:
-                need += len(bits(engines(topo, T.cores[s], core)))
-        for x in sorted({relay(T, topo, s)[0] for s in range(rank) if relay(T, topo, s) and rank in relay(T, topo, s)[1]}):
-            need += len(bits(engines(topo, x, core)))
-        V.wait_ge(S.cin, need)
+        for h in sorted(cwait):
+            V.wait_ge(S["c%d" % h], cwait[h])
         V.tensor_reduce(T.bc[:, 0:1], T.cnt[:, 0:rank], AxisListType.X, A.add).then_inc(S.v, 1)
         V.wait_ge(S.v, 10)
         V.tensor_scalar(T.tt[:], T.psf[:, 0:256], T.bc[:, 0:1], None, A.mult).then_inc(S.v, 1)
@@ -234,14 +240,13 @@ def rank_program(g, core, T, topo):
         V.wait_ge(S.v, 12)
         V.tensor_copy(T.off[:], T.of[:]).then_inc(S.offs, 1)
 
-    ndata = len(bits(near_mask(T, topo, nr)))
+    ndata = len(bits(staying(T, topo, nr)))
     if fr is not None:
         ndata += len(bits(topo.mask(T.cores[fr], core)))
-        ndata += sum(len(pass_on(topo, h, core)) for h in helpers(T, topo, fr))
+        ndata += sum(len(p[3]) for p in split(T, topo, fr))
     for q in (V, g.scalar):
+        q.wait_ge(S.lh, 16)
         q.wait_ge(S.ld, 16)
-        if nh:
-            q.wait_ge(S.lh, 16)
         q.wait_ge(S.lx1, 16)
         q.wait_ge(S.lx2, 16)
         q.wait_ge(S.offs, 1)
@@ -255,45 +260,27 @@ def rank_program(g, core, T, topo):
     last = cuts[-1]
     for c in cuts:
         q, i, a, b = c
-        src = T.win[:, 0:end].indirect(T.off[:, a:b])
+        win = T.win[:, 0:end].indirect(T.off[:, a:b])
         if q == "gv":
-            V.tensor_copy(T.yb[:, 16 * a:16 * b], src).then_inc(S["gv%d" % i], 1)
+            V.tensor_copy(T.yb[:, 16 * a:16 * b], win).then_inc(S["gv%d" % i], 1)
         else:
-            g.scalar.activation(T.yb[:, 16 * a:16 * b], src, ActivationFunctionType.Copy).then_inc(S["ga%d" % i], 1)
+            g.scalar.activation(T.yb[:, 16 * a:16 * b], win, ActivationFunctionType.Copy).then_inc(S["ga%d" % i], 1)
         qq, sm = (g.scalar, S.sz) if c == last else (g.sync, S.sy)
         qq.wait_ge(S["%s%d" % (q, i)], 1)
         qq.dma_start(T.y[:, 16 * a:16 * b], T.yb[:, 16 * a:16 * b]).then_inc(sm, 16)
     g.scalar.wait_ge(S.sz, 16)
     g.sync.wait_ge(S.sy, 16 * (len(cuts) - 1))
-    g.wait_ge(S.sent, nsent[0])
-
-
-def near_mask(T, topo, r):
-    a, b = T.cores[r], T.cores[near(T, topo, r)]
-    return topo.mask(a, b) if far(T, topo, r) is None else engines(topo, a, b)
-
-
-def pass_on(topo, h, dst):
-    return bits(topo.mask(h, dst))[::2]
+    g.wait_ge(S.sent, nsent)
 
 
 def helper_program(g, core, T, topo):
     S = T.sem
-    nsent = [0]
     for r in range(NR):
-        fr = far(T, topo, r)
-        if fr is not None and here(topo, core, T.cores[r]) and core in helpers(T, topo, r):
-            k = helpers(T, topo, r).index(core)
-            to = slot(fr, r) + k * PIECE
-            e = pass_on(topo, core, T.cores[fr])
-            rid, pid = topo.addr(T.cores[fr], core)
-            g.wait_ge(S.hin, 4)
-            g.remote_dma(T.win[:, to:to + PIECE], T.win[:, 0:PIECE], S.data, S.sent, pid, rid, tomask(e))
-            nsent[0] += len(e)
-    src = [s for s in range(NR) if relay(T, topo, s) is not None and relay(T, topo, s)[0] == core]
-    if src:
-        g.wait_ge(S.cin, sum(len(bits(engines(topo, T.cores[s], core))) for s in src))
-        a, b = src[0], src[-1] + 1
-        fan_out(g, T, topo, core, T.cnt[:, a:b], [T.cores[q] for q in relay(T, topo, src[0])[1]], (a, b), nsent)
-    if nsent[0]:
-        g.wait_ge(S.sent, nsent[0])
+        for h, a, b, e in split(T, topo, r):
+            if h == core:
+                f = neighbours(T, topo, r)[0]
+                rid, pid = topo.addr(T.cores[f], core)
+                to = slot(f, r)
+                g.wait_ge(S.hin, 4)
+                g.remote_dma(T.win[:, to + a:to + b], T.win[:, a:b], S.data, S.sent, pid, rid, tomask(e))
+                g.wait_ge(S.sent, len(e))

@@ -3,7 +3,7 @@ from concourse.bass import DstId, RemoteDMATransfer
 from concourse.mybir import dt, AluOpType, AxisListType, ActivationFunctionType
 
 T_, SQ, NR = 4096, 2048, 8
-PC, PS = 384, 256
+PC, PS = (128, 288), (256,)
 CUTS = [40, 48, 40]
 
 SCRATCH = {
@@ -36,7 +36,7 @@ SCRATCH = {
     "psf": ("psum", [128, 512], "float32"),
     "pst": ("psum", [128, 512], "float32"),
 }
-SEMAPHORES = ["lf", "lh", "ld", "lx1", "lx2", "gate", "sent", "data", "hin", "c0", "c1", "c2", "c3",
+SEMAPHORES = ["lf", "lh0", "lh1", "ld", "lx1", "lx2", "gate", "sent", "data", "hin0", "hin1", "c0", "c1", "c2", "c3",
               "vone", "v", "gs", "gj", "fbs", "pcs", "pts", "css", "offs",
               "gv0", "gv1", "gv2", "ga0", "ga1", "ga2", "sy", "sz"]
 
@@ -67,13 +67,16 @@ def neighbours(T, topo, r):
 def split(T, topo, r):
     f = neighbours(T, topo, r)[0]
     if f is None:
-        return []
+        return [], []
     me, to = T.cores[r], T.cores[f]
     w = PS if topo.rack(topo.host(me)) == topo.rack(topo.host(to)) else PC
     chip = [c for c in range(512) if here(topo, c, me)]
     ranks = [c for c in chip if T.rank_of(c) is not None]
     free = [c for c in chip if T.rank_of(c) is None][1 - ranks.index(me)::2]
-    return [(h, k * w, k * w + w, bits(topo.mask(h, to))[::2]) for k, h in enumerate(free)]
+    n = len(free)
+    base = [n * sum(w[i + 1:]) for i in range(len(w))]
+    return ([(h, [(base[i] + k * w[i], base[i] + k * w[i] + w[i]) for i in range(len(w))]) for k, h in enumerate(free)],
+            [(base[i], base[i] + n * w[i]) for i in range(len(w))])
 
 
 def slot(r, i):
@@ -108,9 +111,17 @@ def leaving(topo, a):
     return topo.mask(a, [c for c in range(512) if not here(topo, c, a) and topo.may_write(a, c)][0])
 
 
-def staying(T, topo, r):
-    a, b = T.cores[r], T.cores[neighbours(T, topo, r)[1]]
+def staying(topo, a, b):
     return topo.mask(a, b) & ~leaving(topo, a)
+
+
+def straight(T, topo, r, f):
+    b = bits(topo.mask(T.cores[r], T.cores[f]))
+    return b if topo.rack(topo.host(T.cores[r])) == topo.rack(topo.host(T.cores[f])) else b[:len(b) // 2]
+
+
+def passing(topo, h, far, near):
+    return bits(topo.mask(h, far))[::2], bits(staying(topo, h, near))[::2]
 
 
 def csem(T, topo, s):
@@ -128,6 +139,18 @@ def tell(g, T, topo, core, src, msg):
     return len(bits(m))
 
 
+def feed(g, T, topo, core, pieces, own, wave):
+    on = bits(topo.mask(core, pieces[0][0]))
+    tr = []
+    for k, (h, ab) in enumerate(pieces):
+        rid, pid = topo.addr(h, core)
+        a, b = ab[wave]
+        tr.append(RemoteDMATransfer(dst_ids=[DstId(rid=rid, pnc=pid)], dma_engine_mask=tomask(on[(k + 1) * 4:(k + 2) * 4]),
+                                    remote_sem=T.sem["hin%d" % wave], srcs=[T.win[:, own + a:own + b]], dsts=[T.win[:, a:b]]))
+    g.remote_dma_fused(tr, local_sem=T.sem.sent)
+    return 4 * len(pieces)
+
+
 def rank_program(g, core, T, topo):
     rank = T.rank_of(core)
     if rank is None:
@@ -139,8 +162,7 @@ def rank_program(g, core, T, topo):
     first = max(rank - 1, 0)
     nparts = min(rank + 1, NR - 1) - first + 1
     end = T_ + nparts * SQ
-    pieces = split(T, topo, rank)
-    nh = pieces[-1][2] if pieces else 0
+    pieces, waves = split(T, topo, rank)
     nsent = 0
     ms = messages(T, topo)
     cwait = {}
@@ -149,11 +171,19 @@ def rank_program(g, core, T, topo):
             h = topo.host(T.cores[m[2]])
             cwait[h] = cwait.get(h, 0) + len(bits(leaving(topo, T.cores[m[0]])))
 
+    loads = waves if waves else [(0, SQ // 2)]
+    cut = max(b for a, b in loads)
+    nfirst = waves[-1][1] if waves else 0
+    two = len(loads) > 1
     g.sync.dma_start(T.fi[:], T.fl[:]).then_inc(S.lf, 16)
-    cut = nh if nh else SQ // 2
-    g.scalar.dma_start(T.win[:, own:own + cut], T.st[:, 0:cut]).then_inc(S.lh, 16)
-    g.sync.dma_start(T.win[:, own + cut:own + SQ], T.st[:, cut:SQ]).then_inc(S.ld, 16)
-    g.scalar.dma_start(T.win[:, 0:SQ], T.x[:, 0:SQ]).then_inc(S.lx1, 16)
+    a, b = loads[0]
+    g.scalar.dma_start(T.win[:, own + a:own + b], T.st[:, a:b]).then_inc(S.lh0, 16)
+    if two:
+        a, b = loads[1]
+        g.sync.dma_start(T.win[:, own + a:own + b], T.st[:, a:b]).then_inc(S.lh1, 16)
+    q, qx = (g.scalar, g.sync) if two else (g.sync, g.scalar)
+    q.dma_start(T.win[:, own + cut:own + SQ], T.st[:, cut:SQ]).then_inc(S.ld, 16)
+    qx.dma_start(T.win[:, 0:SQ], T.x[:, 0:SQ]).then_inc(S.lx1, 16)
     g.sync.wait_ge(S.gate, 1)
     g.sync.dma_start(T.win[:, SQ:T_], T.x[:, SQ:T_]).then_inc(S.lx2, 16)
 
@@ -178,30 +208,28 @@ def rank_program(g, core, T, topo):
     V.wait_ge(S.pcs, 1)
     V.tensor_tensor_scan(T.cs[:], T.psc[:, 0:256], T.zero[:], 0.0, A.add, A.add).then_inc(S.css, 1)
 
-    g.wait_ge(S.lh, 16)
+    g.wait_ge(S.lh0, 16)
     if pieces:
-        on = bits(topo.mask(core, pieces[0][0]))
-        tr = []
-        for k, (h, a, b, e) in enumerate(pieces):
-            rid, pid = topo.addr(h, core)
-            q = on[(k + 1) * 4:(k + 2) * 4]
-            tr.append(RemoteDMATransfer(dst_ids=[DstId(rid=rid, pnc=pid)], dma_engine_mask=tomask(q), remote_sem=S.hin,
-                                        srcs=[T.win[:, own + a:own + b]], dsts=[T.win[:, a:b]]))
-            nsent += len(q)
-        g.remote_dma_fused(tr, local_sem=S.sent)
+        nsent += feed(g, T, topo, core, pieces, own, 0)
     for m in ms:
         if m[0] == rank and m[2] == rank:
             g.wait_ge(S.css, 1)
             nsent += tell(g, T, topo, core, T.cs[:, 255:256], m)
     g.wait_ge(S.ld, 16)
-    for q in (fr, nr):
-        if q is not None:
-            m = topo.mask(core, T.cores[q]) if q == fr else staying(T, topo, rank)
-            a = nh if q == fr else 0
-            rid, pid = topo.addr(T.cores[q], core)
-            to = slot(q, rank)
-            g.remote_dma(T.win[:, to + a:to + SQ], T.win[:, own + a:own + SQ], S.data, S.sent, pid, rid, m)
-            nsent += len(bits(m))
+    if fr is not None:
+        e = straight(T, topo, rank, fr)
+        rid, pid = topo.addr(T.cores[fr], core)
+        to = slot(fr, rank)
+        g.remote_dma(T.win[:, to + cut:to + SQ], T.win[:, own + cut:own + SQ], S.data, S.sent, pid, rid, tomask(e))
+        nsent += len(e)
+    if two:
+        g.wait_ge(S.lh1, 16)
+        nsent += feed(g, T, topo, core, pieces, own, 1)
+    m = staying(topo, core, T.cores[nr])
+    rid, pid = topo.addr(T.cores[nr], core)
+    to = slot(nr, rank)
+    g.remote_dma(T.win[:, to + nfirst:to + SQ], T.win[:, own + nfirst:own + SQ], S.data, S.sent, pid, rid, m)
+    nsent += len(bits(m))
     g.sem_inc(S.gate, 1)
     for m in ms:
         if m[0] == rank and m[2] != rank:
@@ -240,12 +268,17 @@ def rank_program(g, core, T, topo):
         V.wait_ge(S.v, 12)
         V.tensor_copy(T.off[:], T.of[:]).then_inc(S.offs, 1)
 
-    ndata = len(bits(staying(T, topo, nr)))
+    ndata = len(bits(staying(topo, T.cores[nr], core)))
+    for h, ab in split(T, topo, nr)[0]:
+        ndata += len(passing(topo, h, T.cores[neighbours(T, topo, nr)[0]], core)[1])
     if fr is not None:
-        ndata += len(bits(topo.mask(T.cores[fr], core)))
-        ndata += sum(len(p[3]) for p in split(T, topo, fr))
+        ndata += len(straight(T, topo, fr, rank))
+        for h, ab in split(T, topo, fr)[0]:
+            ndata += len(ab) * len(passing(topo, h, core, T.cores[neighbours(T, topo, fr)[1]])[0])
     for q in (V, g.scalar):
-        q.wait_ge(S.lh, 16)
+        q.wait_ge(S.lh0, 16)
+        if two:
+            q.wait_ge(S.lh1, 16)
         q.wait_ge(S.ld, 16)
         q.wait_ge(S.lx1, 16)
         q.wait_ge(S.lx2, 16)
@@ -276,11 +309,17 @@ def rank_program(g, core, T, topo):
 def helper_program(g, core, T, topo):
     S = T.sem
     for r in range(NR):
-        for h, a, b, e in split(T, topo, r):
+        for h, ab in split(T, topo, r)[0]:
             if h == core:
-                f = neighbours(T, topo, r)[0]
+                f, n = neighbours(T, topo, r)
+                ef, en = passing(topo, core, T.cores[f], T.cores[n])
                 rid, pid = topo.addr(T.cores[f], core)
                 to = slot(f, r)
-                g.wait_ge(S.hin, 4)
-                g.remote_dma(T.win[:, to + a:to + b], T.win[:, a:b], S.data, S.sent, pid, rid, tomask(e))
-                g.wait_ge(S.sent, len(e))
+                for i, (a, b) in enumerate(ab):
+                    g.wait_ge(S["hin%d" % i], 4)
+                    g.remote_dma(T.win[:, to + a:to + b], T.win[:, a:b], S.data, S.sent, pid, rid, tomask(ef))
+                a, b = ab[-1]
+                rid, pid = topo.addr(T.cores[n], core)
+                to = slot(n, r)
+                g.remote_dma(T.win[:, to + a:to + b], T.win[:, a:b], S.data, S.sent, pid, rid, tomask(en))
+                g.wait_ge(S.sent, len(ab) * len(ef) + len(en))

@@ -3,8 +3,8 @@ from concourse.bass import DstId, RemoteDMATransfer
 from concourse.mybir import dt, AluOpType, AxisListType, ActivationFunctionType
 
 T_, SQ, NR = 4096, 2048, 8
-PC, PS = (128, 288), (256,)
-CUTS = [40, 48, 40]
+PC, PS = (152, 288), (256,)
+CUTS = [24, 44, 40, 20]
 
 SCRATCH = {
     "win": ("sbuf", [128, T_ + 3 * SQ], "bfloat16"),
@@ -38,7 +38,7 @@ SCRATCH = {
 }
 SEMAPHORES = ["lf", "lh0", "lh1", "ld", "lx1", "lx2", "gate", "sent", "data", "hin0", "hin1", "c0", "c1", "c2", "c3",
               "vone", "v", "gs", "gj", "fbs", "pcs", "pts", "css", "offs",
-              "gv0", "gv1", "gv2", "ga0", "ga1", "ga2", "sy", "sz"]
+              "gv0", "gv1", "gv2", "gv3", "ga0", "ga1", "ga2", "ga3", "sy"]
 
 
 def bits(m):
@@ -285,24 +285,16 @@ def rank_program(g, core, T, topo):
         q.wait_ge(S.offs, 1)
         q.wait_ge(S.data, ndata)
     k0 = 0
-    cuts = []
     for i, w in enumerate(CUTS):
-        for q in ("gv", "ga"):
-            cuts.append((q, i, k0, k0 + w))
-            k0 += w
-    last = cuts[-1]
-    for c in cuts:
-        q, i, a, b = c
-        win = T.win[:, 0:end].indirect(T.off[:, a:b])
-        if q == "gv":
-            V.tensor_copy(T.yb[:, 16 * a:16 * b], win).then_inc(S["gv%d" % i], 1)
-        else:
-            g.scalar.activation(T.yb[:, 16 * a:16 * b], win, ActivationFunctionType.Copy).then_inc(S["ga%d" % i], 1)
-        qq, sm = (g.scalar, S.sz) if c == last else (g.sync, S.sy)
-        qq.wait_ge(S["%s%d" % (q, i)], 1)
-        qq.dma_start(T.y[:, 16 * a:16 * b], T.yb[:, 16 * a:16 * b]).then_inc(sm, 16)
-    g.scalar.wait_ge(S.sz, 16)
-    g.sync.wait_ge(S.sy, 16 * (len(cuts) - 1))
+        k1, k2 = k0 + w, k0 + 2 * w
+        V.tensor_copy(T.yb[:, 16 * k0:16 * k1], T.win[:, 0:end].indirect(T.off[:, k0:k1])).then_inc(S["gv%d" % i], 1)
+        g.scalar.activation(T.yb[:, 16 * k1:16 * k2], T.win[:, 0:end].indirect(T.off[:, k1:k2]),
+                            ActivationFunctionType.Copy).then_inc(S["ga%d" % i], 1)
+        g.sync.wait_ge(S["gv%d" % i], 1)
+        g.sync.wait_ge(S["ga%d" % i], 1)
+        g.sync.dma_start(T.y[:, 16 * k0:16 * k2], T.yb[:, 16 * k0:16 * k2]).then_inc(S.sy, 16)
+        k0 = k2
+    g.sync.wait_ge(S.sy, 16 * len(CUTS))
     g.wait_ge(S.sent, nsent)
 
 

import numpy as np
from concourse.bass import DstId, RemoteDMATransfer
from concourse.mybir import dt, AluOpType, AxisListType, ActivationFunctionType

T_, SQ, NR = 4096, 2048, 8
PC, PS = (152, 288), (256,)
CUTS = [24, 44, 40, 20]

SCRATCH = {
    "win": ("sbuf", [128, T_ + 3 * SQ], "bfloat16"),
    "yb": ("sbuf", [128, T_], "bfloat16"),
    "fi": ("sbuf", [16, 256], "int32"),
    "fb": ("sbuf", [16, 256], "bfloat16"),
    "one": ("sbuf", [16, 128], "bfloat16"),
    "neg": ("sbuf", [16, 128], "bfloat16"),
    "rep": ("sbuf", [16, 128], "bfloat16"),
    "low": ("sbuf", [16, 128], "bfloat16"),
    "zero": ("sbuf", [128, 256], "float32"),
    "jq": ("sbuf", [128, 256], "float32"),
    "jj": ("sbuf", [128, 256], "float32"),
    "jk": ("sbuf", [128, 256], "float32"),
    "pi": ("sbuf", [128, 8], "int32"),
    "pj": ("sbuf", [128, 8], "int32"),
    "pf": ("sbuf", [128, 8], "float32"),
    "cs": ("sbuf", [128, 256], "float32"),
    "uu": ("sbuf", [128, 256], "float32"),
    "uv": ("sbuf", [128, 256], "float32"),
    "vv": ("sbuf", [128, 256], "float32"),
    "ww": ("sbuf", [128, 256], "float32"),
    "tt": ("sbuf", [128, 256], "float32"),
    "of": ("sbuf", [128, 256], "float32"),
    "off": ("sbuf", [128, 256], "uint16"),
    "cnt": ("sbuf", [128, 8], "float32"),
    "bc": ("sbuf", [128, 8], "float32"),
    "psc": ("psum", [128, 512], "float32"),
    "psf": ("psum", [128, 512], "float32"),
    "pst": ("psum", [128, 512], "float32"),
}
SEMAPHORES = ["lf", "lh0", "lh1", "ld", "lx1", "lx2", "gate", "sent", "data", "hin0", "hin1", "c0", "c1", "c2", "c3",
              "vone", "v", "gs", "gj", "fbs", "pcs", "pts", "css", "offs",
              "gv0", "gv1", "gv2", "gv3", "ga0", "ga1", "ga2", "ga3", "sy"]


def bits(m):
    return [i for i in range(16) if m >> i & 1]


def tomask(b):
    return int(sum(1 << i for i in b))


def here(topo, a, b):
    return topo.host(a) == topo.host(b) and topo.chip(a) == topo.chip(b)


def neighbours(T, topo, r):
    f = n = None
    for q in (r - 1, r + 1):
        if 0 <= q < NR:
            if here(topo, T.cores[q], T.cores[r]):
                n = q
            else:
                f = q
    return f, n


def split(T, topo, r):
    f = neighbours(T, topo, r)[0]
    if f is None:
        return [], []
    me, to = T.cores[r], T.cores[f]
    w = PS if topo.rack(topo.host(me)) == topo.rack(topo.host(to)) else PC
    chip = [c for c in range(512) if here(topo, c, me)]
    ranks = [c for c in chip if T.rank_of(c) is not None]
    free = [c for c in chip if T.rank_of(c) is None][1 - ranks.index(me)::2]
    n = len(free)
    base = [n * sum(w[i + 1:]) for i in range(len(w))]
    return ([(h, [(base[i] + k * w[i], base[i] + k * w[i] + w[i]) for i in range(len(w))]) for k, h in enumerate(free)],
            [(base[i], base[i] + n * w[i]) for i in range(len(w))])


def slot(r, i):
    return T_ + (i - max(r - 1, 0)) * SQ


def relay(T, topo, s):
    hard = [q for q in range(s + 1, NR) if not topo.may_write(T.cores[s], T.cores[q])]
    if hard:
        for e in range(NR):
            x = T.cores[e]
            if (neighbours(T, topo, e)[0] is None and topo.may_write(T.cores[s], x)
                    and all(topo.may_write(x, T.cores[d]) for d in hard)):
                return e, [q for q in range(s + 1, NR) if q in hard or q != e and here(topo, x, T.cores[q])]
    return None, []


def messages(T, topo):
    ms = []
    for s in range(NR - 1):
        e, served = relay(T, topo, s)
        straight = [q for q in range(s + 1, NR) if q not in served and q != e]
        ms.append((s, ([] if e is None else [e]) + straight, s, s + 1))
    for e in range(NR):
        src = [s for s in range(NR) if relay(T, topo, s)[0] == e]
        if src:
            ms.append((e, sorted(relay(T, topo, src[-1])[1]), src[0], src[-1] + 1))
    return ms


def leaving(topo, a):
    return topo.mask(a, [c for c in range(512) if not here(topo, c, a) and topo.may_write(a, c)][0])


def staying(topo, a, b):
    return topo.mask(a, b) & ~leaving(topo, a)


def straight(T, topo, r, f):
    b = bits(topo.mask(T.cores[r], T.cores[f]))
    return b if topo.rack(topo.host(T.cores[r])) == topo.rack(topo.host(T.cores[f])) else b[:len(b) // 2]


def passing(topo, h, far, near):
    return bits(topo.mask(h, far))[::2], bits(staying(topo, h, near))[::2]


def csem(T, topo, s):
    return T.sem["c%d" % topo.host(T.cores[s])]


def tell(g, T, topo, core, src, msg):
    m = leaving(topo, core)
    ids = []
    for q in msg[1]:
        rid, pid = topo.addr(T.cores[q], core)
        ids.append(DstId(rid=rid, pnc=pid))
    g.remote_dma_fused([RemoteDMATransfer(dst_ids=ids, dma_engine_mask=m, remote_sem=csem(T, topo, msg[2]), srcs=[src],
                                          dsts=[T.cnt[:, msg[2]:msg[3]] for q in ids])], local_sem=T.sem.sent)
    return len(bits(m))


def feed(g, T, topo, core, pieces, own, wave):
    on = bits(topo.mask(core, pieces[0][0]))
    tr = []
    for k, (h, ab) in enumerate(pieces):
        rid, pid = topo.addr(h, core)
        a, b = ab[wave]
        tr.append(RemoteDMATransfer(dst_ids=[DstId(rid=rid, pnc=pid)], dma_engine_mask=tomask(on[(k + 1) * 4:(k + 2) * 4]),
                                    remote_sem=T.sem["hin%d" % wave], srcs=[T.win[:, own + a:own + b]], dsts=[T.win[:, a:b]]))
    g.remote_dma_fused(tr, local_sem=T.sem.sent)
    return 4 * len(pieces)


def rank_program(g, core, T, topo):
    rank = T.rank_of(core)
    if rank is None:
        helper_program(g, core, T, topo)
        return
    S, A, V, PE = T.sem, AluOpType, g.vector, g.tensor
    fr, nr = neighbours(T, topo, rank)
    own = slot(rank, rank)
    first = max(rank - 1, 0)
    nparts = min(rank + 1, NR - 1) - first + 1
    end = T_ + nparts * SQ
    pieces, waves = split(T, topo, rank)
    nsent = 0
    ms = messages(T, topo)
    cwait = {}
    for m in ms:
        if rank in m[1]:
            h = topo.host(T.cores[m[2]])
            cwait[h] = cwait.get(h, 0) + len(bits(leaving(topo, T.cores[m[0]])))

    loads = waves if waves else [(0, SQ // 2)]
    cut = max(b for a, b in loads)
    nfirst = waves[-1][1] if waves else 0
    two = len(loads) > 1
    g.sync.dma_start(T.fi[:], T.fl[:]).then_inc(S.lf, 16)
    a, b = loads[0]
    g.scalar.dma_start(T.win[:, own + a:own + b], T.st[:, a:b]).then_inc(S.lh0, 16)
    if two:
        a, b = loads[1]
        g.sync.dma_start(T.win[:, own + a:own + b], T.st[:, a:b]).then_inc(S.lh1, 16)
    q, qx = (g.scalar, g.sync) if two else (g.sync, g.scalar)
    q.dma_start(T.win[:, own + cut:own + SQ], T.st[:, cut:SQ]).then_inc(S.ld, 16)
    qx.dma_start(T.win[:, 0:SQ], T.x[:, 0:SQ]).then_inc(S.lx1, 16)
    g.sync.wait_ge(S.gate, 1)
    g.sync.dma_start(T.win[:, SQ:T_], T.x[:, SQ:T_]).then_inc(S.lx2, 16)

    V.memset(T.one[:], 1.0).then_inc(S.vone, 1)
    V.memset(T.neg[:], -1.0).then_inc(S.vone, 1)
    V.memset(T.zero[:], 0.0).then_inc(S.v, 1)
    g.wait_ge(S.vone, 2)
    g.affine_select(T.rep[:], T.one[:], [[0, 8], [-1, 16]], A.is_equal, 0.0, 0, 1).then_inc(S.gs, 1)
    g.affine_select(T.low[:], T.neg[:], [[0, 8], [-1, 16]], A.is_ge, 0.0, 0, 1).then_inc(S.gs, 1)
    g.iota(T.pi[:, 0:1], [[0, 1]], 0, 1).then_inc(S.gj, 1)
    g.iota(T.jq[:], [[16, 256]], 0, 0, allow_small_or_imprecise_dtypes=True).then_inc(S.gj, 1)

    V.wait_ge(S.lf, 16)
    V.tensor_copy(T.fb[:], T.fi[:]).then_inc(S.fbs, 1)
    PE.wait_ge(S.vone, 2)
    PE.wait_ge(S.fbs, 1)
    PE.matmul(T.psc[:, 0:256], T.one[:], T.fb[:], True, True).then_inc(S.pcs, 1)
    PE.wait_ge(S.gs, 2)
    PE.matmul(T.psf[:, 0:256], T.rep[:], T.fb[:], True, True).then_inc(S.pts, 1)
    PE.matmul(T.pst[:, 0:256], T.low[:], T.fb[:], True, True).then_inc(S.pts, 1)
    V.wait_ge(S.v, 1)
    V.wait_ge(S.pcs, 1)
    V.tensor_tensor_scan(T.cs[:], T.psc[:, 0:256], T.zero[:], 0.0, A.add, A.add).then_inc(S.css, 1)

    g.wait_ge(S.lh0, 16)
    if pieces:
        nsent += feed(g, T, topo, core, pieces, own, 0)
    for m in ms:
        if m[0] == rank and m[2] == rank:
            g.wait_ge(S.css, 1)
            nsent += tell(g, T, topo, core, T.cs[:, 255:256], m)
    g.wait_ge(S.ld, 16)
    if fr is not None:
        e = straight(T, topo, rank, fr)
        rid, pid = topo.addr(T.cores[fr], core)
        to = slot(fr, rank)
        g.remote_dma(T.win[:, to + cut:to + SQ], T.win[:, own + cut:own + SQ], S.data, S.sent, pid, rid, tomask(e))
        nsent += len(e)
    if two:
        g.wait_ge(S.lh1, 16)
        nsent += feed(g, T, topo, core, pieces, own, 1)
    m = staying(topo, core, T.cores[nr])
    rid, pid = topo.addr(T.cores[nr], core)
    to = slot(nr, rank)
    g.remote_dma(T.win[:, to + nfirst:to + SQ], T.win[:, own + nfirst:own + SQ], S.data, S.sent, pid, rid, m)
    nsent += len(bits(m))
    g.sem_inc(S.gate, 1)
    for m in ms:
        if m[0] == rank and m[2] != rank:
            g.wait_ge(csem(T, topo, m[2]), cwait[topo.host(T.cores[m[2]])])
            nsent += tell(g, T, topo, core, T.cnt[:, m[2]:m[3]], m)

    K = T_ - SQ * first
    V.wait_ge(S.gj, 2)
    V.tensor_scalar(T.pj[:, 0:1], T.pi[:, 0:1], 15, None, A.bitwise_and).then_inc(S.v, 1)
    V.wait_ge(S.v, 2)
    V.tensor_copy(T.pf[:, 0:1], T.pj[:, 0:1]).then_inc(S.v, 1)
    V.wait_ge(S.v, 3)
    V.tensor_scalar(T.jj[:], T.jq[:], T.pf[:, 0:1], None, A.add).then_inc(S.v, 1)
    V.tensor_scalar(T.jk[:], T.jq[:], T.pf[:, 0:1], float(-K), A.add, A.add).then_inc(S.v, 1)
    V.wait_ge(S.v, 5)
    V.wait_ge(S.pts, 2)
    V.wait_ge(S.css, 1)
    V.tensor_tensor(T.uu[:], T.pst[:, 0:256], T.jk[:], A.subtract).then_inc(S.v, 1)
    V.wait_ge(S.v, 6)
    V.tensor_tensor(T.uv[:], T.uu[:], T.cs[:], A.add).then_inc(S.v, 1)
    V.wait_ge(S.v, 7)
    V.tensor_tensor(T.vv[:], T.uv[:], T.psf[:, 0:256], A.mult).then_inc(S.v, 1)
    V.wait_ge(S.v, 8)
    V.tensor_tensor(T.ww[:], T.vv[:], T.jj[:], A.add).then_inc(S.v, 1)
    V.wait_ge(S.v, 9)
    if rank == 0:
        V.tensor_copy(T.off[:], T.ww[:]).then_inc(S.offs, 1)
    else:
        for h in sorted(cwait):
            V.wait_ge(S["c%d" % h], cwait[h])
        V.tensor_reduce(T.bc[:, 0:1], T.cnt[:, 0:rank], AxisListType.X, A.add).then_inc(S.v, 1)
        V.wait_ge(S.v, 10)
        V.tensor_scalar(T.tt[:], T.psf[:, 0:256], T.bc[:, 0:1], None, A.mult).then_inc(S.v, 1)
        V.wait_ge(S.v, 11)
        V.tensor_tensor(T.of[:], T.tt[:], T.ww[:], A.add).then_inc(S.v, 1)
        V.wait_ge(S.v, 12)
        V.tensor_copy(T.off[:], T.of[:]).then_inc(S.offs, 1)

    ndata = len(bits(staying(topo, T.cores[nr], core)))
    for h, ab in split(T, topo, nr)[0]:
        ndata += len(passing(topo, h, T.cores[neighbours(T, topo, nr)[0]], core)[1])
    if fr is not None:
        ndata += len(straight(T, topo, fr, rank))
        for h, ab in split(T, topo, fr)[0]:
            ndata += len(ab) * len(passing(topo, h, core, T.cores[neighbours(T, topo, fr)[1]])[0])
    for q in (V, g.scalar):
        q.wait_ge(S.lh0, 16)
        if two:
            q.wait_ge(S.lh1, 16)
        q.wait_ge(S.ld, 16)
        q.wait_ge(S.lx1, 16)
        q.wait_ge(S.lx2, 16)
        q.wait_ge(S.offs, 1)
        q.wait_ge(S.data, ndata)
    k0 = 0
    for i, w in enumerate(CUTS):
        k1, k2 = k0 + w, k0 + 2 * w
        V.tensor_copy(T.yb[:, 16 * k0:16 * k1], T.win[:, 0:end].indirect(T.off[:, k0:k1])).then_inc(S["gv%d" % i], 1)
        g.scalar.activation(T.yb[:, 16 * k1:16 * k2], T.win[:, 0:end].indirect(T.off[:, k1:k2]),
                            ActivationFunctionType.Copy).then_inc(S["ga%d" % i], 1)
        g.sync.wait_ge(S["gv%d" % i], 1)
        g.sync.wait_ge(S["ga%d" % i], 1)
        g.sync.dma_start(T.y[:, 16 * k0:16 * k2], T.yb[:, 16 * k0:16 * k2]).then_inc(S.sy, 16)
        k0 = k2
    g.sync.wait_ge(S.sy, 16 * len(CUTS))
    g.wait_ge(S.sent, nsent)


def helper_program(g, core, T, topo):
    S = T.sem
    for r in range(NR):
        for h, ab in split(T, topo, r)[0]:
            if h == core:
                f, n = neighbours(T, topo, r)
                ef, en = passing(topo, core, T.cores[f], T.cores[n])
                rid, pid = topo.addr(T.cores[f], core)
                to = slot(f, r)
                for i, (a, b) in enumerate(ab):
                    g.wait_ge(S["hin%d" % i], 4)
                    g.remote_dma(T.win[:, to + a:to + b], T.win[:, a:b], S.data, S.sent, pid, rid, tomask(ef))
                a, b = ab[-1]
                rid, pid = topo.addr(T.cores[n], core)
                to = slot(n, r)
                g.remote_dma(T.win[:, to + a:to + b], T.win[:, a:b], S.data, S.sent, pid, rid, tomask(en))
                g.wait_ge(S.sent, len(ab) * len(ef) + len(en))
